import numpy as np, ml_dtypes
CORES = [0,1,2,3,4,5,6,7]
N = 8
ROOT = 5
def setup_inputs(rng):
    return {"x": rng.standard_normal((N, 128, 8192), dtype=np.float32).astype(ml_dtypes.bfloat16)}
def reference(x):
    return {"y": np.broadcast_to(x[ROOT], x.shape)}

@@ -1,0 +1,29 @@
+from concourse.bass import DstId, RemoteDMATransfer
+
+SCRATCH = {
+    "buf": ("sbuf", [128, 8192], "bfloat16"),
+}
+SEMAPHORES = ["loaded", "read", "arrived", "stored"]
+
+
+def rank_program(g, core, T, topo):
+    rank = T.rank_of(core)
+    if rank is None:
+        return
+    root = T.cores[T.root]
+    if core == root:
+        g.dma_start(T.buf[:], T.x[:]).then_inc(T.sem.loaded, 16)
+        g.dma_start(T.y[:], T.x[:]).then_inc(T.sem.stored, 16)
+        g.wait_ge(T.sem.loaded, 16)
+        others = [c for c in T.cores if c != root]
+        ids = [DstId(rid=topo.addr(c)[0], pnc=topo.addr(c)[1]) for c in others]
+        g.remote_dma_fused(
+            [RemoteDMATransfer(dst_ids=ids, dma_engine_mask=0xFFFF, remote_sem=T.sem.arrived,
+                               src=T.buf[:], dsts=[T.buf[:] for c in others])],
+            local_sem=T.sem.read)
+        g.wait_ge(T.sem.read, 16)
+        g.wait_ge(T.sem.stored, 16)
+    else:
+        g.wait_ge(T.sem.arrived, 16)
+        g.dma_start(T.y[:], T.buf[:]).then_inc(T.sem.stored, 16)
+        g.wait_ge(T.sem.stored, 16)

@@ -3,27 +3,81 @@ from concourse.bass import DstId, RemoteDMATransfer
 SCRATCH = {
     "buf": ("sbuf", [128, 8192], "bfloat16"),
 }
-SEMAPHORES = ["loaded", "read", "arrived", "stored"]
+SEMAPHORES = ["ld0", "ld1", "ld2", "stored", "sent", "t0", "t1", "t2", "q0", "q1", "q2"]
+
+SLICE = [688, 688, 672]
+ALL_ENGINES = 0xFFFF
+QUARTER_ENGINES = [0x000F, 0x00F0, 0x0F00, 0xF000]
 
 
 def rank_program(g, core, T, topo):
-    rank = T.rank_of(core)
-    if rank is None:
+    if T.rank_of(core) is None:
         return
     root = T.cores[T.root]
+    near = [c for c in T.cores if c != root and topo.die(c) == topo.die(root)]
+    far = [c for c in T.cores if topo.die(c) != topo.die(root)]
+    thirds = range(len(SLICE))
+    t = [T.sem.t0, T.sem.t1, T.sem.t2]
+    q = [T.sem.q0, T.sem.q1, T.sem.q2]
+
+    start = [4 * sum(SLICE[:j]) for j in thirds]
+
+    def third(tensor, j):
+        return tensor[:, start[j]:start[j] + 4 * SLICE[j]]
+
+    def piece(j, k):
+        a = start[j] + k * SLICE[j]
+        return T.buf[:, a:a + SLICE[j]]
+
+    def dst(c):
+        rid, pid, ring = topo.addr(c)
+        return DstId(rid=rid, pnc=pid)
+
     if core == root:
-        g.dma_start(T.buf[:], T.x[:]).then_inc(T.sem.loaded, 16)
+        ld = [T.sem.ld0, T.sem.ld1, T.sem.ld2]
+        for j in thirds:
+            g.dma_start(third(T.buf, j), third(T.x, j)).then_inc(ld[j], 16)
+        for j in thirds:
+            g.wait_ge(ld[j], 16)
+            rid, pid, ring = topo.addr(near[j])
+            g.remote_dma(third(T.buf, j), third(T.buf, j), remote_sem=t[j], local_sem=T.sem.sent,
+                         pid=pid, routing_id=rid, dma_engine_mask=ALL_ENGINES)
         g.dma_start(T.y[:], T.x[:]).then_inc(T.sem.stored, 16)
-        g.wait_ge(T.sem.loaded, 16)
-        others = [c for c in T.cores if c != root]
-        ids = [DstId(rid=topo.addr(c)[0], pnc=topo.addr(c)[1]) for c in others]
+        g.wait_ge(T.sem.sent, 16 * len(SLICE))
+        g.wait_ge(T.sem.stored, 16)
+        return
+
+    if core in near:
+        me = near.index(core)
+        g.wait_ge(t[me], 16)
         g.remote_dma_fused(
-            [RemoteDMATransfer(dst_ids=ids, dma_engine_mask=0xFFFF, remote_sem=T.sem.arrived,
-                               src=T.buf[:], dsts=[T.buf[:] for c in others])],
-            local_sem=T.sem.read)
-        g.wait_ge(T.sem.read, 16)
-        g.wait_ge(T.sem.stored, 16)
-    else:
-        g.wait_ge(T.sem.arrived, 16)
-        g.dma_start(T.y[:], T.buf[:]).then_inc(T.sem.stored, 16)
-        g.wait_ge(T.sem.stored, 16)
+            [RemoteDMATransfer(dst_ids=[dst(far[k])], dma_engine_mask=QUARTER_ENGINES[k], remote_sem=t[me],
+                               src=piece(me, k), dst=piece(me, k)) for k in range(len(far))],
+            local_sem=T.sem.sent)
+        peers = [c for c in near if c != core]
+        g.remote_dma_fused(
+            [RemoteDMATransfer(dst_ids=[dst(c) for c in peers], dma_engine_mask=ALL_ENGINES, remote_sem=t[me],
+                               src=third(T.buf, me), dsts=[third(T.buf, me) for c in peers])],
+            local_sem=T.sem.sent)
+        g.dma_start(third(T.y, me), third(T.buf, me)).then_inc(T.sem.stored, 16)
+        for j in thirds:
+            if j != me:
+                g.wait_ge(t[j], 16)
+                g.dma_start(third(T.y, j), third(T.buf, j)).then_inc(T.sem.stored, 16)
+        g.wait_ge(T.sem.sent, 16 + 16)
+        g.wait_ge(T.sem.stored, 16 * len(SLICE))
+        return
+
+    me = far.index(core)
+    peers = [c for c in far if c != core]
+    for j in thirds:
+        g.wait_ge(t[j], 4)
+        g.remote_dma_fused(
+            [RemoteDMATransfer(dst_ids=[dst(c) for c in peers], dma_engine_mask=ALL_ENGINES, remote_sem=q[j],
+                               src=piece(j, me), dsts=[piece(j, me) for c in peers])],
+            local_sem=T.sem.sent)
+    for j in thirds:
+        g.wait_ge(q[j], 16 * len(peers))
+        g.dma_start(third(T.y, j), third(T.buf, j)).then_inc(T.sem.stored, 16)
+    g.wait_ge(T.sem.sent, 16 * len(SLICE))
+    g.wait_ge(T.sem.stored, 16 * len(SLICE))

from concourse.bass import DstId, RemoteDMATransfer

SCRATCH = {
    "buf": ("sbuf", [128, 8192], "bfloat16"),
}
SEMAPHORES = ["ld0", "ld1", "ld2", "stored", "sent", "t0", "t1", "t2", "q0", "q1", "q2"]

SLICE = [688, 688, 672]
ALL_ENGINES = 0xFFFF
QUARTER_ENGINES = [0x000F, 0x00F0, 0x0F00, 0xF000]


def rank_program(g, core, T, topo):
    if T.rank_of(core) is None:
        return
    root = T.cores[T.root]
    near = [c for c in T.cores if c != root and topo.die(c) == topo.die(root)]
    far = [c for c in T.cores if topo.die(c) != topo.die(root)]
    thirds = range(len(SLICE))
    t = [T.sem.t0, T.sem.t1, T.sem.t2]
    q = [T.sem.q0, T.sem.q1, T.sem.q2]

    start = [4 * sum(SLICE[:j]) for j in thirds]

    def third(tensor, j):
        return tensor[:, start[j]:start[j] + 4 * SLICE[j]]

    def piece(j, k):
        a = start[j] + k * SLICE[j]
        return T.buf[:, a:a + SLICE[j]]

    def dst(c):
        rid, pid, ring = topo.addr(c)
        return DstId(rid=rid, pnc=pid)

    if core == root:
        ld = [T.sem.ld0, T.sem.ld1, T.sem.ld2]
        for j in thirds:
            g.dma_start(third(T.buf, j), third(T.x, j)).then_inc(ld[j], 16)
        for j in thirds:
            g.wait_ge(ld[j], 16)
            rid, pid, ring = topo.addr(near[j])
            g.remote_dma(third(T.buf, j), third(T.buf, j), remote_sem=t[j], local_sem=T.sem.sent,
                         pid=pid, routing_id=rid, dma_engine_mask=ALL_ENGINES)
        g.dma_start(T.y[:], T.x[:]).then_inc(T.sem.stored, 16)
        g.wait_ge(T.sem.sent, 16 * len(SLICE))
        g.wait_ge(T.sem.stored, 16)
        return

    if core in near:
        me = near.index(core)
        g.wait_ge(t[me], 16)
        g.remote_dma_fused(
            [RemoteDMATransfer(dst_ids=[dst(far[k])], dma_engine_mask=QUARTER_ENGINES[k], remote_sem=t[me],
                               src=piece(me, k), dst=piece(me, k)) for k in range(len(far))],
            local_sem=T.sem.sent)
        peers = [c for c in near if c != core]
        g.remote_dma_fused(
            [RemoteDMATransfer(dst_ids=[dst(c) for c in peers], dma_engine_mask=ALL_ENGINES, remote_sem=t[me],
                               src=third(T.buf, me), dsts=[third(T.buf, me) for c in peers])],
            local_sem=T.sem.sent)
        g.dma_start(third(T.y, me), third(T.buf, me)).then_inc(T.sem.stored, 16)
        for j in thirds:
            if j != me:
                g.wait_ge(t[j], 16)
                g.dma_start(third(T.y, j), third(T.buf, j)).then_inc(T.sem.stored, 16)
        g.wait_ge(T.sem.sent, 16 + 16)
        g.wait_ge(T.sem.stored, 16 * len(SLICE))
        return

    me = far.index(core)
    peers = [c for c in far if c != core]
    for j in thirds:
        g.wait_ge(t[j], 4)
        g.remote_dma_fused(
            [RemoteDMATransfer(dst_ids=[dst(c) for c in peers], dma_engine_mask=ALL_ENGINES, remote_sem=q[j],
                               src=piece(j, me), dsts=[piece(j, me) for c in peers])],
            local_sem=T.sem.sent)
    for j in thirds:
        g.wait_ge(q[j], 16 * len(peers))
        g.dma_start(third(T.y, j), third(T.buf, j)).then_inc(T.sem.stored, 16)
    g.wait_ge(T.sem.sent, 16 * len(SLICE))
    g.wait_ge(T.sem.stored, 16 * len(SLICE))
